import numpy as np
import ml_dtypes


def mxq(x, axis, fmt="e4m3"):
    dtype, down = {"e4m3": (ml_dtypes.float8_e4m3fn, 7), "e5m2": (ml_dtypes.float8_e5m2, 14)}[fmt]
    v = np.moveaxis(np.asarray(x, np.float32).astype(ml_dtypes.bfloat16).astype(np.float64), axis, -1)
    blocks = v.reshape(v.shape[:-1] + (-1, 32))
    amax = np.abs(blocks).max(-1, keepdims=True)
    byte = np.maximum(np.where(amax > 0, np.frexp(amax)[1] - 1 + 127, 0) - down, 1)
    scale = np.exp2(byte - 127.0)
    codes = (blocks / scale).astype(np.float32).astype(dtype).astype(np.float64)
    return np.moveaxis((codes * scale).reshape(v.shape), -1, axis)


WIDE = False


def mx_kscale(k):
    if not WIDE:
        return np.ones(k)
    levels = np.array([10, -10, 5, -5, 0])
    if k % 512:
        return np.exp2(np.random.permutation(np.resize(levels, k // 32))).repeat(32)
    a = np.empty((k // 512, 16))
    for p in range(k // 512):
        a[p, :8] = np.random.permutation(np.resize(levels, 8))
        for g in range(8):
            far = levels[np.abs(levels - a[p, g]) >= 10]
            a[p, g + 8] = far[np.random.randint(len(far))]
    return np.exp2(a.ravel()).repeat(32)


def f64(x):
    return np.asarray(x).astype(np.float64)


def striped(idx):
    return np.tile(idx.reshape(-1, 16).T, (8, 1)).astype(np.uint16)


def unstriped(offs):
    return offs[:16].T.reshape(-1).astype(np.int64)


K, T, E, C, N = 2048, 512, 4, 256, 128


def by_expert(wq, xq):
    return np.concatenate([wq[e].T @ xq[:, e * C:(e + 1) * C] for e in range(E)], axis=1)


def setup_inputs():
    n = np.random.standard_normal
    s = mx_kscale(K)[:, None]
    first = np.random.permutation(np.repeat(np.arange(E), T // E))
    second = (first + 1 + np.random.permutation(np.repeat(np.arange(E - 1), -(-T // (E - 1)))[:T])) % E
    while np.bincount(second, minlength=E).max() != T // E:
        load = np.bincount(second, minlength=E); hi, lo = int(load.argmax()), int(load.argmin())
        t = np.flatnonzero((second == hi) & (first != lo))[0]; second[t] = lo
    slot_token = np.empty(E * C, np.int64); pos = np.empty((2, T), np.int64); fill = np.zeros(E, np.int64)
    place = np.stack([np.random.permutation(C) for _ in range(E)])
    for r, deal in enumerate((first, second)):
        for t in np.random.permutation(T):
            e = deal[t]; j = e * C + place[e, fill[e]]; fill[e] += 1; slot_token[j] = t; pos[r, t] = j
    g = np.random.uniform(0.2, 0.8, T)
    return {
        "xT": (n((K, T)) * s).astype(np.float32),
        "w": (n((E, K, N)) / np.sqrt(K) / s[None]).astype(np.float32),
        "gate": np.stack([np.tile(g, (N, 1)), np.tile(1.0 - g, (N, 1))]).astype(np.float32),
        "offs": striped(slot_token),
        "pos1": striped(pos[0]),
        "pos2": striped(pos[1]),
    }


def reference(xT, w, gate, offs, pos1, pos2):
    idx = unstriped(offs)
    xq = mxq(f64(xT)[:, idx], 0, "e4m3")
    y = by_expert(mxq(f64(w), 1, "e4m3"), xq)
    return f64(gate[0]) * y[:, unstriped(pos1)] + f64(gate[1]) * y[:, unstriped(pos2)]

@@ -1,0 +1,150 @@
+from contextlib import ExitStack
+
+import concourse.mybir as mybir
+
+K, T, E, C, N = 2048, 512, 4, 256, 128
+FLOPS = 2 * K * N * E * C
+
+F32 = mybir.dt.float32
+BF16 = mybir.dt.bfloat16
+U32 = mybir.dt.uint32
+U16 = mybir.dt.uint16
+U8 = mybir.dt.uint8
+FP8X4 = mybir.dt.float8_e4m3fn_x4
+MULT = mybir.AluOpType.mult
+ADD = mybir.AluOpType.add
+COPY = mybir.ActivationFunctionType.Copy
+
+P = 128
+PASSES = K // 512
+SLOTS = E * C
+
+V_PASSES = (0, 2)
+S_PASSES = (1, 3)
+W_ON_VECTOR = (0, 1, 2)
+
+
+def tile_routed_moe_kernel(tc, xT, w, gate, offs, pos1, pos2, out):
+    nc = tc.nc
+    with ExitStack() as ctx:
+        lists = ctx.enter_context(tc.tile_pool(name="lists", bufs=1))
+        keep = ctx.enter_context(tc.tile_pool(name="keep", bufs=1))
+        psum = ctx.enter_context(tc.psum_pool(name="psum", bufs=1))
+
+        offs_t = lists.tile([P, SLOTS // 16], U16, name="offs_t")
+        pos1_t = lists.tile([P, T // 16], U16, name="pos1_t")
+        pos2_t = lists.tile([P, T // 16], U16, name="pos2_t")
+        nc.sync.dma_start(offs_t[:], offs)
+
+        x_view = xT.rearrange("(g p j) n -> g p j n", g=PASSES, p=P, j=4)
+        w_view = w.rearrange("e (g p j) n -> g p e (j n)", g=PASSES, p=P, j=4)
+        raw = [keep.tile([P, 4, T], F32, name="raw%d" % g) for g in range(PASSES)]
+        wraw = [keep.tile([P, E, 4 * N], F32, name="wraw%d" % g) for g in range(PASSES)]
+        for j in range(4):
+            nc.sync.dma_start(raw[V_PASSES[0]][:, j, :], x_view[V_PASSES[0], :, j, :])
+            nc.sync.dma_start(raw[S_PASSES[0]][:, j, :], x_view[S_PASSES[0], :, j, :])
+        nc.sync.dma_start(raw[V_PASSES[1]][:], x_view[V_PASSES[1]])
+        nc.sync.dma_start(raw[S_PASSES[1]][:], x_view[S_PASSES[1]])
+        for g in range(PASSES):
+            nc.sync.dma_start(wraw[g][:], w_view[g])
+        gate_t = keep.tile([P, 2, T], F32, name="gate_t")
+        nc.sync.dma_start(gate_t[:], gate.rearrange("r n t -> n r t"))
+        nc.sync.dma_start(pos1_t[:], pos1)
+        nc.sync.dma_start(pos2_t[:], pos2)
+
+        zero = keep.tile([P, 1], F32, name="zero")
+        warm = keep.tile([P, 1], F32, name="warm")
+        nc.vector.memset(zero[:], 0.0)
+        nc.scalar.copy(warm[:], zero[:])
+
+        xb = {}
+        for g in S_PASSES:
+            xb[g] = keep.tile([P, 4, T], BF16, name="xb%d" % g)
+        quad = [keep.tile([P, SLOTS, 4], BF16, name="quad%d" % g, align_bytes=64) for g in range(PASSES)]
+        wquad = [keep.tile([P, 4 * E * N], BF16, name="wquad%d" % g, align_bytes=64) for g in range(PASSES)]
+        x_codes = keep.tile([P, PASSES, SLOTS], U32, name="x_codes", align_bytes=64)
+        x_scales = keep.tile([P, PASSES, SLOTS], U8, name="x_scales", align_bytes=64)
+        w_codes = keep.tile([P, PASSES, E * N], U32, name="w_codes", align_bytes=64)
+        w_scales = keep.tile([P, PASSES, E * N], U8, name="w_scales", align_bytes=64)
+        acc = [psum.tile([P, C], F32, name="acc%d" % e) for e in range(E)]
+        y = keep.tile([P, SLOTS], F32, name="y")
+
+        def gather(g, e, j):
+            dst = quad[g][:, e * C : (e + 1) * C, j]
+            cols = offs_t[:, e * C // 16 : (e + 1) * C // 16]
+            if g in V_PASSES:
+                nc.vector.tensor_copy(dst, raw[g][:, j, :].indirect(cols))
+            else:
+                nc.scalar.activation(dst, xb[g][:, j, :].indirect(cols), COPY)
+
+        def quant_x(g, a, b):
+            nc.vector.quantize_mx(
+                out=x_codes[:, g, a:b].bitcast(FP8X4),
+                scales=x_scales[:, g, a:b],
+                in_=quad[g][:, a:b, :].rearrange("p n j -> p (n j)"),
+            )
+
+        def prep_w(g):
+            dst = wquad[g][:].rearrange("p (e n j) -> p e n j", e=E, j=4)
+            src = wraw[g][:].rearrange("p e (j n) -> p e n j", j=4)
+            if g in W_ON_VECTOR:
+                nc.vector.tensor_copy(dst, src)
+            else:
+                nc.scalar.copy(dst, src)
+
+        def quant_w(g):
+            nc.vector.quantize_mx(
+                out=w_codes[:, g, :].bitcast(FP8X4),
+                scales=w_scales[:, g, :],
+                in_=wquad[g][:],
+            )
+
+        order = (V_PASSES[0], S_PASSES[0], V_PASSES[1], S_PASSES[1])
+
+        def multiply(g, e):
+            nc.tensor.matmul_mx(
+                out=acc[e][:],
+                lhsT=w_codes[:, g, e * N : (e + 1) * N].bitcast(FP8X4),
+                lhsT_scale=w_scales[:, g, e * N : (e + 1) * N],
+                rhs=x_codes[:, g, e * C : (e + 1) * C].bitcast(FP8X4),
+                rhs_scale=x_scales[:, g, e * C : (e + 1) * C],
+                start=(g == order[0]),
+                stop=(g == order[-1]),
+            )
+
+        for j in range(4):
+            nc.scalar.copy(xb[S_PASSES[0]][:, j, :], raw[S_PASSES[0]][:, j, :])
+            for e in range(E):
+                gather(V_PASSES[0], e, j)
+                gather(S_PASSES[0], e, j)
+        nc.scalar.copy(xb[S_PASSES[1]][:], raw[S_PASSES[1]][:])
+        for g in range(PASSES):
+            prep_w(g)
+        quant_x(V_PASSES[0], 0, SLOTS)
+        for g in range(PASSES):
+            quant_w(g)
+        quant_x(S_PASSES[0], 0, SLOTS)
+        for g in order[:2]:
+            for e in range(E):
+                multiply(g, e)
+        for e in range(E):
+            for j in range(4):
+                gather(V_PASSES[1], e, j)
+                gather(S_PASSES[1], e, j)
+            if e > 0:
+                for g in order[2:]:
+                    quant_x(g, (e - 1) * C, e * C)
+                    multiply(g, e - 1)
+                nc.scalar.copy(y[:, (e - 1) * C : e * C], acc[e - 1][:])
+        for g in order[2:]:
+            quant_x(g, (E - 1) * C, E * C)
+            multiply(g, E - 1)
+        nc.scalar.copy(y[:, (E - 1) * C : E * C], acc[E - 1][:])
+
+        part1 = keep.tile([P, T], F32, name="part1")
+        part2 = keep.tile([P, T], F32, name="part2")
+        total = keep.tile([P, T], F32, name="total")
+        nc.vector.tensor_tensor(part1[:], y[:].indirect(pos1_t[:]), gate_t[:, 0, :], MULT)
+        nc.vector.tensor_tensor(part2[:], y[:].indirect(pos2_t[:]), gate_t[:, 1, :], MULT)
+        nc.vector.tensor_tensor(total[:], part1[:], part2[:], ADD)
+        nc.sync.dma_start(out, total[:])

@@ -21,7 +21,6 @@ SLOTS = E * C
 
 V_PASSES = (0, 2)
 S_PASSES = (1, 3)
-W_ON_VECTOR = (0, 1, 2)
 
 
 def tile_routed_moe_kernel(tc, xT, w, gate, offs, pos1, pos2, out):
@@ -43,10 +42,12 @@ def tile_routed_moe_kernel(tc, xT, w, gate, offs, pos1, pos2, out):
         for j in range(4):
             nc.sync.dma_start(raw[V_PASSES[0]][:, j, :], x_view[V_PASSES[0], :, j, :])
             nc.sync.dma_start(raw[S_PASSES[0]][:, j, :], x_view[S_PASSES[0], :, j, :])
+        nc.sync.dma_start(wraw[0][:], w_view[0])
+        nc.sync.dma_start(wraw[1][:], w_view[1])
         nc.sync.dma_start(raw[V_PASSES[1]][:], x_view[V_PASSES[1]])
         nc.sync.dma_start(raw[S_PASSES[1]][:], x_view[S_PASSES[1]])
-        for g in range(PASSES):
-            nc.sync.dma_start(wraw[g][:], w_view[g])
+        nc.sync.dma_start(wraw[2][:], w_view[2])
+        nc.sync.dma_start(wraw[3][:], w_view[3])
         gate_t = keep.tile([P, 2, T], F32, name="gate_t")
         nc.sync.dma_start(gate_t[:], gate.rearrange("r n t -> n r t"))
         nc.sync.dma_start(pos1_t[:], pos1)
@@ -87,10 +88,8 @@ def tile_routed_moe_kernel(tc, xT, w, gate, offs, pos1, pos2, out):
         def prep_w(g):
             dst = wquad[g][:].rearrange("p (e n j) -> p e n j", e=E, j=4)
             src = wraw[g][:].rearrange("p e (j n) -> p e n j", j=4)
-            if g in W_ON_VECTOR:
-                nc.vector.tensor_copy(dst, src)
-            else:
-                nc.scalar.copy(dst, src)
+            for e in range(E):
+                nc.gpsimd.tensor_scalar(dst[:, e], src[:, e], 1.0, 0.0, MULT, ADD)
 
         def quant_w(g):
             nc.vector.quantize_mx(

@@ -40,8 +40,8 @@ def tile_routed_moe_kernel(tc, xT, w, gate, offs, pos1, pos2, out):
         raw = [keep.tile([P, 4, T], F32, name="raw%d" % g) for g in range(PASSES)]
         wraw = [keep.tile([P, E, 4 * N], F32, name="wraw%d" % g) for g in range(PASSES)]
         for j in range(4):
-            nc.sync.dma_start(raw[V_PASSES[0]][:, j, :], x_view[V_PASSES[0], :, j, :])
             nc.sync.dma_start(raw[S_PASSES[0]][:, j, :], x_view[S_PASSES[0], :, j, :])
+            nc.sync.dma_start(raw[V_PASSES[0]][:, j, :], x_view[V_PASSES[0], :, j, :])
         nc.sync.dma_start(wraw[0][:], w_view[0])
         nc.sync.dma_start(wraw[1][:], w_view[1])
         nc.sync.dma_start(raw[V_PASSES[1]][:], x_view[V_PASSES[1]])
@@ -58,9 +58,7 @@ def tile_routed_moe_kernel(tc, xT, w, gate, offs, pos1, pos2, out):
         nc.vector.memset(zero[:], 0.0)
         nc.scalar.copy(warm[:], zero[:])
 
-        xb = {}
-        for g in S_PASSES:
-            xb[g] = keep.tile([P, 4, T], BF16, name="xb%d" % g)
+        xb = [keep.tile([P, 2, T], BF16, name="xb%d" % j) for j in range(4)]
         quad = [keep.tile([P, SLOTS, 4], BF16, name="quad%d" % g, align_bytes=64) for g in range(PASSES)]
         wquad = [keep.tile([P, 4 * E * N], BF16, name="wquad%d" % g, align_bytes=64) for g in range(PASSES)]
         x_codes = keep.tile([P, PASSES, SLOTS], U32, name="x_codes", align_bytes=64)
@@ -76,7 +74,10 @@ def tile_routed_moe_kernel(tc, xT, w, gate, offs, pos1, pos2, out):
             if g in V_PASSES:
                 nc.vector.tensor_copy(dst, raw[g][:, j, :].indirect(cols))
             else:
-                nc.scalar.activation(dst, xb[g][:, j, :].indirect(cols), COPY)
+                nc.scalar.activation(dst, xb[j][:, S_PASSES.index(g), :].indirect(cols), COPY)
+
+        def cast(g, j):
+            nc.gpsimd.tensor_scalar(xb[j][:, S_PASSES.index(g), :], raw[g][:, j, :], 1.0, 0.0, MULT, ADD)
 
         def quant_x(g, a, b):
             nc.vector.quantize_mx(
@@ -112,13 +113,16 @@ def tile_routed_moe_kernel(tc, xT, w, gate, offs, pos1, pos2, out):
             )
 
         for j in range(4):
-            nc.scalar.copy(xb[S_PASSES[0]][:, j, :], raw[S_PASSES[0]][:, j, :])
+            cast(S_PASSES[0], j)
             for e in range(E):
                 gather(V_PASSES[0], e, j)
                 gather(S_PASSES[0], e, j)
-        nc.scalar.copy(xb[S_PASSES[1]][:], raw[S_PASSES[1]][:])
-        for g in range(PASSES):
-            prep_w(g)
+        prep_w(0)
+        prep_w(1)
+        for j in range(4):
+            cast(S_PASSES[1], j)
+        prep_w(2)
+        prep_w(3)
         quant_x(V_PASSES[0], 0, SLOTS)
         for g in range(PASSES):
             quant_w(g)

@@ -19,15 +19,13 @@ P = 128
 PASSES = K // 512
 SLOTS = E * C
 
-V_PASSES = (0, 2)
-S_PASSES = (1, 3)
-
 
 def tile_routed_moe_kernel(tc, xT, w, gate, offs, pos1, pos2, out):
     nc = tc.nc
     with ExitStack() as ctx:
         lists = ctx.enter_context(tc.tile_pool(name="lists", bufs=1))
         keep = ctx.enter_context(tc.tile_pool(name="keep", bufs=1))
+        ring = ctx.enter_context(tc.tile_pool(name="ring", bufs=2))
         psum = ctx.enter_context(tc.psum_pool(name="psum", bufs=1))
 
         offs_t = lists.tile([P, SLOTS // 16], U16, name="offs_t")
@@ -40,12 +38,12 @@ def tile_routed_moe_kernel(tc, xT, w, gate, offs, pos1, pos2, out):
         raw = [keep.tile([P, 4, T], F32, name="raw%d" % g) for g in range(PASSES)]
         wraw = [keep.tile([P, E, 4 * N], F32, name="wraw%d" % g) for g in range(PASSES)]
         for j in range(4):
-            nc.sync.dma_start(raw[S_PASSES[0]][:, j, :], x_view[S_PASSES[0], :, j, :])
-            nc.sync.dma_start(raw[V_PASSES[0]][:, j, :], x_view[V_PASSES[0], :, j, :])
-        nc.sync.dma_start(wraw[0][:], w_view[0])
+            nc.sync.dma_start(raw[1][:, j, :], x_view[1, :, j, :])
+            nc.sync.dma_start(raw[0][:, j, :], x_view[0, :, j, :])
+            nc.sync.dma_start(wraw[0][:, j, :], w_view[0, :, j, :])
         nc.sync.dma_start(wraw[1][:], w_view[1])
-        nc.sync.dma_start(raw[V_PASSES[1]][:], x_view[V_PASSES[1]])
-        nc.sync.dma_start(raw[S_PASSES[1]][:], x_view[S_PASSES[1]])
+        nc.sync.dma_start(raw[2][:], x_view[2])
+        nc.sync.dma_start(raw[3][:], x_view[3])
         nc.sync.dma_start(wraw[2][:], w_view[2])
         nc.sync.dma_start(wraw[3][:], w_view[3])
         gate_t = keep.tile([P, 2, T], F32, name="gate_t")
@@ -58,91 +56,94 @@ def tile_routed_moe_kernel(tc, xT, w, gate, offs, pos1, pos2, out):
         nc.vector.memset(zero[:], 0.0)
         nc.scalar.copy(warm[:], zero[:])
 
-        xb = [keep.tile([P, 2, T], BF16, name="xb%d" % j) for j in range(4)]
-        quad = [keep.tile([P, SLOTS, 4], BF16, name="quad%d" % g, align_bytes=64) for g in range(PASSES)]
+        xb = {1: keep.tile([P, 4, T], BF16, name="xb1"), 3: keep.tile([P, 4, T], BF16, name="xb3")}
+        quad = [keep.tile([P, 4 * SLOTS], BF16, name="quad%d" % g, align_bytes=64) for g in range(PASSES)]
         wquad = [keep.tile([P, 4 * E * N], BF16, name="wquad%d" % g, align_bytes=64) for g in range(PASSES)]
         x_codes = keep.tile([P, PASSES, SLOTS], U32, name="x_codes", align_bytes=64)
         x_scales = keep.tile([P, PASSES, SLOTS], U8, name="x_scales", align_bytes=64)
-        w_codes = keep.tile([P, PASSES, E * N], U32, name="w_codes", align_bytes=64)
         w_scales = keep.tile([P, PASSES, E * N], U8, name="w_scales", align_bytes=64)
         acc = [psum.tile([P, C], F32, name="acc%d" % e) for e in range(E)]
         y = keep.tile([P, SLOTS], F32, name="y")
 
-        def gather(g, e, j):
-            dst = quad[g][:, e * C : (e + 1) * C, j]
+        def pair_tile(tag, slots):
+            return ring.tile([P, 2, 2 * slots], BF16, name=tag, tag=tag, align_bytes=64)
+
+        def gather(g, pairs, first, e, j):
+            dst = pairs[:, j // 2, :].rearrange("p (n i) -> p n i", i=2)[:, e * C - first : (e + 1) * C - first, j % 2]
             cols = offs_t[:, e * C // 16 : (e + 1) * C // 16]
-            if g in V_PASSES:
+            if g in (0, 2):
                 nc.vector.tensor_copy(dst, raw[g][:, j, :].indirect(cols))
             else:
-                nc.scalar.activation(dst, xb[j][:, S_PASSES.index(g), :].indirect(cols), COPY)
+                nc.scalar.activation(dst, xb[g][:, j, :].indirect(cols), COPY)
 
-        def cast(g, j):
-            nc.gpsimd.tensor_scalar(xb[j][:, S_PASSES.index(g), :], raw[g][:, j, :], 1.0, 0.0, MULT, ADD)
+        def merge(g, pairs, a, b):
+            dst = quad[g][:].bitcast(F32)[:, 2 * a : 2 * b].rearrange("p (n u) -> p n u", u=2)
+            src = pairs[:].bitcast(F32).rearrange("p u n -> p n u")
+            if g in (0, 2):
+                nc.vector.tensor_copy(dst, src)
+            else:
+                nc.scalar.copy(dst, src)
 
         def quant_x(g, a, b):
             nc.vector.quantize_mx(
                 out=x_codes[:, g, a:b].bitcast(FP8X4),
                 scales=x_scales[:, g, a:b],
-                in_=quad[g][:, a:b, :].rearrange("p n j -> p (n j)"),
+                in_=quad[g][:, 4 * a : 4 * b],
             )
 
         def prep_w(g):
             dst = wquad[g][:].rearrange("p (e n j) -> p e n j", e=E, j=4)
             src = wraw[g][:].rearrange("p e (j n) -> p e n j", j=4)
-            for e in range(E):
-                nc.gpsimd.tensor_scalar(dst[:, e], src[:, e], 1.0, 0.0, MULT, ADD)
+            if g == PASSES - 1:
+                nc.scalar.copy(dst, src)
+            else:
+                for e in range(E):
+                    nc.gpsimd.tensor_scalar(dst[:, e], src[:, e], 1.0, 0.0, MULT, ADD)
 
-        def quant_w(g):
+        for g in range(PASSES):
+            prep_w(g)
+        first_v = pair_tile("vpair", SLOTS)
+        first_s = pair_tile("spair", SLOTS)
+        for j in range(4):
+            nc.scalar.copy(xb[1][:, j, :], raw[1][:, j, :])
+            for e in range(E):
+                gather(1, first_s, 0, e, j)
+                gather(0, first_v, 0, e, j)
+        merge(0, first_v, 0, SLOTS)
+        merge(1, first_s, 0, SLOTS)
+        nc.scalar.copy(xb[3][:], raw[3][:])
+        quant_x(0, 0, SLOTS)
+        quant_x(1, 0, SLOTS)
+        for e in range(E):
+            unit_v = pair_tile("vpair", C)
+            unit_s = pair_tile("spair", C)
+            for j in range(4):
+                gather(3, unit_s, e * C, e, j)
+                gather(2, unit_v, e * C, e, j)
+            merge(2, unit_v, e * C, (e + 1) * C)
+            merge(3, unit_s, e * C, (e + 1) * C)
+            quant_x(2, e * C, (e + 1) * C)
+            quant_x(3, e * C, (e + 1) * C)
+
+        w_codes = ring.tile([P, PASSES, E * N], U32, name="vpair", tag="vpair", align_bytes=64)
+        for g in range(PASSES):
             nc.vector.quantize_mx(
                 out=w_codes[:, g, :].bitcast(FP8X4),
                 scales=w_scales[:, g, :],
                 in_=wquad[g][:],
             )
-
-        order = (V_PASSES[0], S_PASSES[0], V_PASSES[1], S_PASSES[1])
-
-        def multiply(g, e):
-            nc.tensor.matmul_mx(
-                out=acc[e][:],
-                lhsT=w_codes[:, g, e * N : (e + 1) * N].bitcast(FP8X4),
-                lhsT_scale=w_scales[:, g, e * N : (e + 1) * N],
-                rhs=x_codes[:, g, e * C : (e + 1) * C].bitcast(FP8X4),
-                rhs_scale=x_scales[:, g, e * C : (e + 1) * C],
-                start=(g == order[0]),
-                stop=(g == order[-1]),
-            )
-
-        for j in range(4):
-            cast(S_PASSES[0], j)
             for e in range(E):
-                gather(V_PASSES[0], e, j)
-                gather(S_PASSES[0], e, j)
-        prep_w(0)
-        prep_w(1)
-        for j in range(4):
-            cast(S_PASSES[1], j)
-        prep_w(2)
-        prep_w(3)
-        quant_x(V_PASSES[0], 0, SLOTS)
-        for g in range(PASSES):
-            quant_w(g)
-        quant_x(S_PASSES[0], 0, SLOTS)
-        for g in order[:2]:
-            for e in range(E):
-                multiply(g, e)
+                nc.tensor.matmul_mx(
+                    out=acc[e][:],
+                    lhsT=w_codes[:, g, e * N : (e + 1) * N].bitcast(FP8X4),
+                    lhsT_scale=w_scales[:, g, e * N : (e + 1) * N],
+                    rhs=x_codes[:, g, e * C : (e + 1) * C].bitcast(FP8X4),
+                    rhs_scale=x_scales[:, g, e * C : (e + 1) * C],
+                    start=(g == 0),
+                    stop=(g == PASSES - 1),
+                )
         for e in range(E):
-            for j in range(4):
-                gather(V_PASSES[1], e, j)
-                gather(S_PASSES[1], e, j)
-            if e > 0:
-                for g in order[2:]:
-                    quant_x(g, (e - 1) * C, e * C)
-                    multiply(g, e - 1)
-                nc.scalar.copy(y[:, (e - 1) * C : e * C], acc[e - 1][:])
-        for g in order[2:]:
-            quant_x(g, (E - 1) * C, E * C)
-            multiply(g, E - 1)
-        nc.scalar.copy(y[:, (E - 1) * C : E * C], acc[E - 1][:])
+            nc.scalar.copy(y[:, e * C : (e + 1) * C], acc[e][:])
 
         part1 = keep.tile([P, T], F32, name="part1")
         part2 = keep.tile([P, T], F32, name="part2")

@@ -25,7 +25,6 @@ def tile_routed_moe_kernel(tc, xT, w, gate, offs, pos1, pos2, out):
     with ExitStack() as ctx:
         lists = ctx.enter_context(tc.tile_pool(name="lists", bufs=1))
         keep = ctx.enter_context(tc.tile_pool(name="keep", bufs=1))
-        ring = ctx.enter_context(tc.tile_pool(name="ring", bufs=2))
         psum = ctx.enter_context(tc.psum_pool(name="psum", bufs=1))
 
         offs_t = lists.tile([P, SLOTS // 16], U16, name="offs_t")
@@ -37,13 +36,31 @@ def tile_routed_moe_kernel(tc, xT, w, gate, offs, pos1, pos2, out):
         w_view = w.rearrange("e (g p j) n -> g p e (j n)", g=PASSES, p=P, j=4)
         raw = [keep.tile([P, 4, T], F32, name="raw%d" % g) for g in range(PASSES)]
         wraw = [keep.tile([P, E, 4 * N], F32, name="wraw%d" % g) for g in range(PASSES)]
-        for j in range(4):
-            nc.sync.dma_start(raw[1][:, j, :], x_view[1, :, j, :])
-            nc.sync.dma_start(raw[0][:, j, :], x_view[0, :, j, :])
-            nc.sync.dma_start(wraw[0][:, j, :], w_view[0, :, j, :])
+
+        def load_x(g, j):
+            nc.sync.dma_start(raw[g][:, j, :], x_view[g, :, j, :])
+
+        def load_w0(e):
+            nc.sync.dma_start(wraw[0][:, e, :], w_view[0, :, e, :])
+
+        load_x(1, 0)
+        load_x(1, 1)
+        load_x(0, 0)
+        load_w0(0)
+        load_x(1, 2)
+        load_x(0, 1)
+        load_w0(1)
+        load_x(1, 3)
+        load_x(3, 0)
+        load_x(0, 2)
+        load_w0(2)
+        load_x(3, 1)
+        load_x(0, 3)
+        load_w0(3)
         nc.sync.dma_start(wraw[1][:], w_view[1])
+        load_x(3, 2)
+        load_x(3, 3)
         nc.sync.dma_start(raw[2][:], x_view[2])
-        nc.sync.dma_start(raw[3][:], x_view[3])
         nc.sync.dma_start(wraw[2][:], w_view[2])
         nc.sync.dma_start(wraw[3][:], w_view[3])
         gate_t = keep.tile([P, 2, T], F32, name="gate_t")
@@ -56,7 +73,9 @@ def tile_routed_moe_kernel(tc, xT, w, gate, offs, pos1, pos2, out):
         nc.vector.memset(zero[:], 0.0)
         nc.scalar.copy(warm[:], zero[:])
 
-        xb = {1: keep.tile([P, 4, T], BF16, name="xb1"), 3: keep.tile([P, 4, T], BF16, name="xb3")}
+        xb = {}
+        for g in (1, 2, 3):
+            xb[g] = keep.tile([P, 4, T], BF16, name="xb%d" % g)
         quad = [keep.tile([P, 4 * SLOTS], BF16, name="quad%d" % g, align_bytes=64) for g in range(PASSES)]
         wquad = [keep.tile([P, 4 * E * N], BF16, name="wquad%d" % g, align_bytes=64) for g in range(PASSES)]
         x_codes = keep.tile([P, PASSES, SLOTS], U32, name="x_codes", align_bytes=64)
@@ -65,24 +84,19 @@ def tile_routed_moe_kernel(tc, xT, w, gate, offs, pos1, pos2, out):
         acc = [psum.tile([P, C], F32, name="acc%d" % e) for e in range(E)]
         y = keep.tile([P, SLOTS], F32, name="y")
 
-        def pair_tile(tag, slots):
-            return ring.tile([P, 2, 2 * slots], BF16, name=tag, tag=tag, align_bytes=64)
-
-        def gather(g, pairs, first, e, j):
+        def gather(engine, g, pairs, first, e, j):
             dst = pairs[:, j // 2, :].rearrange("p (n i) -> p n i", i=2)[:, e * C - first : (e + 1) * C - first, j % 2]
             cols = offs_t[:, e * C // 16 : (e + 1) * C // 16]
-            if g in (0, 2):
+            if engine == "vector":
                 nc.vector.tensor_copy(dst, raw[g][:, j, :].indirect(cols))
             else:
                 nc.scalar.activation(dst, xb[g][:, j, :].indirect(cols), COPY)
 
         def merge(g, pairs, a, b):
-            dst = quad[g][:].bitcast(F32)[:, 2 * a : 2 * b].rearrange("p (n u) -> p n u", u=2)
-            src = pairs[:].bitcast(F32).rearrange("p u n -> p n u")
-            if g in (0, 2):
-                nc.vector.tensor_copy(dst, src)
-            else:
-                nc.scalar.copy(dst, src)
+            nc.vector.tensor_copy(
+                quad[g][:].bitcast(F32)[:, 2 * a : 2 * b].rearrange("p (n u) -> p n u", u=2),
+                pairs[:].bitcast(F32).rearrange("p u n -> p n u"),
+            )
 
         def quant_x(g, a, b):
             nc.vector.quantize_mx(
@@ -95,54 +109,75 @@ def tile_routed_moe_kernel(tc, xT, w, gate, offs, pos1, pos2, out):
             dst = wquad[g][:].rearrange("p (e n j) -> p e n j", e=E, j=4)
             src = wraw[g][:].rearrange("p e (j n) -> p e n j", j=4)
             if g == PASSES - 1:
-                nc.scalar.copy(dst, src)
+                nc.vector.tensor_copy(dst, src)
             else:
                 for e in range(E):
                     nc.gpsimd.tensor_scalar(dst[:, e], src[:, e], 1.0, 0.0, MULT, ADD)
 
-        for g in range(PASSES):
+        for g in range(PASSES - 1):
             prep_w(g)
-        first_v = pair_tile("vpair", SLOTS)
-        first_s = pair_tile("spair", SLOTS)
-        for j in range(4):
-            nc.scalar.copy(xb[1][:, j, :], raw[1][:, j, :])
-            for e in range(E):
-                gather(1, first_s, 0, e, j)
-                gather(0, first_v, 0, e, j)
-        merge(0, first_v, 0, SLOTS)
-        merge(1, first_s, 0, SLOTS)
-        nc.scalar.copy(xb[3][:], raw[3][:])
-        quant_x(0, 0, SLOTS)
-        quant_x(1, 0, SLOTS)
-        for e in range(E):
-            unit_v = pair_tile("vpair", C)
-            unit_s = pair_tile("spair", C)
-            for j in range(4):
-                gather(3, unit_s, e * C, e, j)
-                gather(2, unit_v, e * C, e, j)
-            merge(2, unit_v, e * C, (e + 1) * C)
-            merge(3, unit_s, e * C, (e + 1) * C)
-            quant_x(2, e * C, (e + 1) * C)
-            quant_x(3, e * C, (e + 1) * C)
 
-        w_codes = ring.tile([P, PASSES, E * N], U32, name="vpair", tag="vpair", align_bytes=64)
+        pairs1 = keep.tile([P, 2, 2 * SLOTS], BF16, name="pairs1")
+        pairs0 = keep.tile([P, 2, 2 * SLOTS], BF16, name="pairs0")
+        pairs3 = keep.tile([P, 2, 2 * SLOTS], BF16, name="pairs3", tag="late", align_bytes=64)
+        for j in range(4):
+            nc.vector.tensor_copy(xb[1][:, j, :], raw[1][:, j, :])
+            for e in range(E):
+                gather("scalar", 1, pairs1, 0, e, j)
+        for j in range(4):
+            for e in range(E):
+                gather("vector", 0, pairs0, 0, e, j)
+        for j in range(4):
+            nc.vector.tensor_copy(xb[3][:, j, :], raw[3][:, j, :])
+            for e in range(E):
+                gather("scalar", 3, pairs3, 0, e, j)
+        merge(1, pairs1, 0, SLOTS)
+        nc.vector.tensor_copy(xb[2][:], raw[2][:])
+        units = [keep.tile([P, 2, 2 * C], BF16, name="unit%d" % e) for e in range(E)]
+        for j in range(4):
+            gather("vector", 2, units[3], 3 * C, 3, j)
+        merge(0, pairs0, 0, SLOTS)
+        quant_x(1, 0, SLOTS)
+        prep_w(3)
+        merge(2, units[3], 3 * C, 4 * C)
+        quant_x(0, 0, SLOTS)
+        for j in (0, 1):
+            gather("vector", 2, units[2], 2 * C, 2, j)
+        for e in range(3):
+            for j in range(4):
+                if e < 2 or j > 1:
+                    gather("scalar", 2, units[e], e * C, e, j)
+        merge(3, pairs3, 0, SLOTS)
+        quant_x(2, 3 * C, 4 * C)
+
+        w_codes = keep.tile([P, PASSES, E * N], U32, name="w_codes", tag="late", align_bytes=64)
+
+        def multiply(g, e, first, last):
+            nc.tensor.matmul_mx(
+                out=acc[e][:],
+                lhsT=w_codes[:, g, e * N : (e + 1) * N].bitcast(FP8X4),
+                lhsT_scale=w_scales[:, g, e * N : (e + 1) * N],
+                rhs=x_codes[:, g, e * C : (e + 1) * C].bitcast(FP8X4),
+                rhs_scale=x_scales[:, g, e * C : (e + 1) * C],
+                start=first,
+                stop=last,
+            )
+
         for g in range(PASSES):
             nc.vector.quantize_mx(
                 out=w_codes[:, g, :].bitcast(FP8X4),
                 scales=w_scales[:, g, :],
                 in_=wquad[g][:],
             )
+        quant_x(3, 0, SLOTS)
+        for g in (0, 1, 3):
             for e in range(E):
-                nc.tensor.matmul_mx(
-                    out=acc[e][:],
-                    lhsT=w_codes[:, g, e * N : (e + 1) * N].bitcast(FP8X4),
-                    lhsT_scale=w_scales[:, g, e * N : (e + 1) * N],
-                    rhs=x_codes[:, g, e * C : (e + 1) * C].bitcast(FP8X4),
-                    rhs_scale=x_scales[:, g, e * C : (e + 1) * C],
-                    start=(g == 0),
-                    stop=(g == PASSES - 1),
-                )
-        for e in range(E):
+                multiply(g, e, g == 0, False)
+        for e in (3, 0, 1, 2):
+            if e < 3:
+                merge(2, units[e], e * C, (e + 1) * C)
+                quant_x(2, e * C, (e + 1) * C)
+            multiply(2, e, False, True)
             nc.scalar.copy(y[:, e * C : (e + 1) * C], acc[e][:])
 
         part1 = keep.tile([P, T], F32, name="part1")

@@ -19,6 +19,9 @@ P = 128
 PASSES = K // 512
 SLOTS = E * C
 
+W_PIECE = 128
+SCALAR_LOW = (0, 1)
+X_ORDER = ((1, 0), (1, 1), (0, 0), (1, 2), (1, 3), (3, 0), (3, 1), (3, 2), (3, 3), (2, 0), (2, 1), (2, 2), (2, 3), (0, 1), (0, 2), (0, 3))
 
 def tile_routed_moe_kernel(tc, xT, w, gate, offs, pos1, pos2, out):
     nc = tc.nc
@@ -34,35 +37,23 @@ def tile_routed_moe_kernel(tc, xT, w, gate, offs, pos1, pos2, out):
 
         x_view = xT.rearrange("(g p j) n -> g p j n", g=PASSES, p=P, j=4)
         w_view = w.rearrange("e (g p j) n -> g p e (j n)", g=PASSES, p=P, j=4)
-        raw = [keep.tile([P, 4, T], F32, name="raw%d" % g) for g in range(PASSES)]
+        raw = {}
+        for g in (0, 1, 3):
+            raw[g] = keep.tile([P, 4, T], F32, name="raw%d" % g)
+        raw[2] = keep.tile([P, 4, T], F32, name="raw2", tag="slot_a", align_bytes=64)
         wraw = [keep.tile([P, E, 4 * N], F32, name="wraw%d" % g) for g in range(PASSES)]
 
         def load_x(g, j):
             nc.sync.dma_start(raw[g][:, j, :], x_view[g, :, j, :])
 
-        def load_w0(e):
-            nc.sync.dma_start(wraw[0][:, e, :], w_view[0, :, e, :])
+        def load_w(g):
+            for e in range(E):
+                nc.sync.dma_start(wraw[g][:, e, :], w_view[g, :, e, :])
 
-        load_x(1, 0)
-        load_x(1, 1)
-        load_x(0, 0)
-        load_w0(0)
-        load_x(1, 2)
-        load_x(0, 1)
-        load_w0(1)
-        load_x(1, 3)
-        load_x(3, 0)
-        load_x(0, 2)
-        load_w0(2)
-        load_x(3, 1)
-        load_x(0, 3)
-        load_w0(3)
-        nc.sync.dma_start(wraw[1][:], w_view[1])
-        load_x(3, 2)
-        load_x(3, 3)
-        nc.sync.dma_start(raw[2][:], x_view[2])
-        nc.sync.dma_start(wraw[2][:], w_view[2])
-        nc.sync.dma_start(wraw[3][:], w_view[3])
+        for g, j in X_ORDER:
+            load_x(g, j)
+        for g in range(PASSES):
+            load_w(g)
         gate_t = keep.tile([P, 2, T], F32, name="gate_t")
         nc.sync.dma_start(gate_t[:], gate.rearrange("r n t -> n r t"))
         nc.sync.dma_start(pos1_t[:], pos1)
@@ -76,26 +67,43 @@ def tile_routed_moe_kernel(tc, xT, w, gate, offs, pos1, pos2, out):
         xb = {}
         for g in (1, 2, 3):
             xb[g] = keep.tile([P, 4, T], BF16, name="xb%d" % g)
-        quad = [keep.tile([P, 4 * SLOTS], BF16, name="quad%d" % g, align_bytes=64) for g in range(PASSES)]
+        quad = {}
+        quad[0] = keep.tile([P, 4 * SLOTS], BF16, name="quad0", align_bytes=64)
+        quad[2] = keep.tile([P, 4 * SLOTS], BF16, name="quad2", align_bytes=64)
         wquad = [keep.tile([P, 4 * E * N], BF16, name="wquad%d" % g, align_bytes=64) for g in range(PASSES)]
         x_codes = keep.tile([P, PASSES, SLOTS], U32, name="x_codes", align_bytes=64)
         x_scales = keep.tile([P, PASSES, SLOTS], U8, name="x_scales", align_bytes=64)
         w_scales = keep.tile([P, PASSES, E * N], U8, name="w_scales", align_bytes=64)
         acc = [psum.tile([P, C], F32, name="acc%d" % e) for e in range(E)]
         y = keep.tile([P, SLOTS], F32, name="y")
+        pairs = {}
+        for g in (0, 1):
+            pairs[g] = keep.tile([P, 2, 2 * SLOTS], BF16, name="pairs%d" % g)
+        pairs[3] = keep.tile([P, 2, 2 * SLOTS], BF16, name="pairs3", tag="slot_b", align_bytes=64)
+        units = [keep.tile([P, 2, 2 * C], BF16, name="unit%d" % e) for e in range(E)]
 
-        def gather(engine, g, pairs, first, e, j):
-            dst = pairs[:, j // 2, :].rearrange("p (n i) -> p n i", i=2)[:, e * C - first : (e + 1) * C - first, j % 2]
+        def cast(g, j):
+            nc.vector.tensor_copy(xb[g][:, j, :], raw[g][:, j, :])
+
+        def gather(engine, g, e, j):
+            if g == 2:
+                dst = units[e][:, j // 2, :].rearrange("p (n i) -> p n i", i=2)[:, :, j % 2]
+            else:
+                dst = pairs[g][:, j // 2, :].rearrange("p (n i) -> p n i", i=2)[:, e * C : (e + 1) * C, j % 2]
             cols = offs_t[:, e * C // 16 : (e + 1) * C // 16]
             if engine == "vector":
                 nc.vector.tensor_copy(dst, raw[g][:, j, :].indirect(cols))
             else:
                 nc.scalar.activation(dst, xb[g][:, j, :].indirect(cols), COPY)
 
-        def merge(g, pairs, a, b):
+        def plane(engine, g, j):
+            for e in range(E):
+                gather(engine, g, e, j)
+
+        def merge(g, src, a, b):
             nc.vector.tensor_copy(
                 quad[g][:].bitcast(F32)[:, 2 * a : 2 * b].rearrange("p (n u) -> p n u", u=2),
-                pairs[:].bitcast(F32).rearrange("p u n -> p n u"),
+                src[:].bitcast(F32).rearrange("p u n -> p n u"),
             )
 
         def quant_x(g, a, b):
@@ -108,49 +116,46 @@ def tile_routed_moe_kernel(tc, xT, w, gate, offs, pos1, pos2, out):
         def prep_w(g):
             dst = wquad[g][:].rearrange("p (e n j) -> p e n j", e=E, j=4)
             src = wraw[g][:].rearrange("p e (j n) -> p e n j", j=4)
-            if g == PASSES - 1:
-                nc.vector.tensor_copy(dst, src)
-            else:
-                for e in range(E):
-                    nc.gpsimd.tensor_scalar(dst[:, e], src[:, e], 1.0, 0.0, MULT, ADD)
+            for e in range(E):
+                for h in range(0, N, W_PIECE):
+                    nc.gpsimd.tensor_scalar(dst[:, e, h : h + W_PIECE], src[:, e, h : h + W_PIECE], 1.0, 0.0, MULT, ADD)
 
-        for g in range(PASSES - 1):
+        for g in range(PASSES):
             prep_w(g)
 
-        pairs1 = keep.tile([P, 2, 2 * SLOTS], BF16, name="pairs1")
-        pairs0 = keep.tile([P, 2, 2 * SLOTS], BF16, name="pairs0")
-        pairs3 = keep.tile([P, 2, 2 * SLOTS], BF16, name="pairs3", tag="late", align_bytes=64)
-        for j in range(4):
-            nc.vector.tensor_copy(xb[1][:, j, :], raw[1][:, j, :])
-            for e in range(E):
-                gather("scalar", 1, pairs1, 0, e, j)
-        for j in range(4):
-            for e in range(E):
-                gather("vector", 0, pairs0, 0, e, j)
-        for j in range(4):
-            nc.vector.tensor_copy(xb[3][:, j, :], raw[3][:, j, :])
-            for e in range(E):
-                gather("scalar", 3, pairs3, 0, e, j)
-        merge(1, pairs1, 0, SLOTS)
-        nc.vector.tensor_copy(xb[2][:], raw[2][:])
-        units = [keep.tile([P, 2, 2 * C], BF16, name="unit%d" % e) for e in range(E)]
-        for j in range(4):
-            gather("vector", 2, units[3], 3 * C, 3, j)
-        merge(0, pairs0, 0, SLOTS)
-        quant_x(1, 0, SLOTS)
-        prep_w(3)
-        merge(2, units[3], 3 * C, 4 * C)
-        quant_x(0, 0, SLOTS)
-        for j in (0, 1):
-            gather("vector", 2, units[2], 2 * C, 2, j)
-        for e in range(3):
+        for g, j in X_ORDER:
+            if g == 0:
+                plane("vector", 0, j)
+            elif g == 2:
+                if j > 1 or SCALAR_LOW:
+                    cast(2, j)
+            else:
+                cast(g, j)
+                plane("scalar", g, j)
+        for e in range(E):
             for j in range(4):
-                if e < 2 or j > 1:
-                    gather("scalar", 2, units[e], e * C, e, j)
-        merge(3, pairs3, 0, SLOTS)
-        quant_x(2, 3 * C, 4 * C)
+                if j > 1 or e in SCALAR_LOW:
+                    gather("scalar", 2, e, j)
+        for e in range(E):
+            for j in (0, 1):
+                if e not in SCALAR_LOW:
+                    gather("vector", 2, e, j)
 
-        w_codes = keep.tile([P, PASSES, E * N], U32, name="w_codes", tag="late", align_bytes=64)
+        merge(0, pairs[0], 0, SLOTS)
+        quad[1] = keep.tile([P, 4 * SLOTS], BF16, name="quad1", tag="slot_a", align_bytes=64)
+        merge(1, pairs[1], 0, SLOTS)
+        quant_x(0, 0, SLOTS)
+        quant_x(1, 0, SLOTS)
+        quad[3] = keep.tile([P, 4 * SLOTS], BF16, name="quad3", tag="slot_a", align_bytes=64)
+        merge(3, pairs[3], 0, SLOTS)
+        quant_x(3, 0, SLOTS)
+        w_codes = keep.tile([P, PASSES, E * N], U32, name="w_codes", tag="slot_b", align_bytes=64)
+        for g in range(PASSES):
+            nc.vector.quantize_mx(
+                out=w_codes[:, g, :].bitcast(FP8X4),
+                scales=w_scales[:, g, :],
+                in_=wquad[g][:],
+            )
 
         def multiply(g, e, first, last):
             nc.tensor.matmul_mx(
@@ -163,20 +168,12 @@ def tile_routed_moe_kernel(tc, xT, w, gate, offs, pos1, pos2, out):
                 stop=last,
             )
 
-        for g in range(PASSES):
-            nc.vector.quantize_mx(
-                out=w_codes[:, g, :].bitcast(FP8X4),
-                scales=w_scales[:, g, :],
-                in_=wquad[g][:],
-            )
-        quant_x(3, 0, SLOTS)
         for g in (0, 1, 3):
             for e in range(E):
                 multiply(g, e, g == 0, False)
-        for e in (3, 0, 1, 2):
-            if e < 3:
-                merge(2, units[e], e * C, (e + 1) * C)
-                quant_x(2, e * C, (e + 1) * C)
+        for e in range(E):
+            merge(2, units[e], e * C, (e + 1) * C)
+            quant_x(2, e * C, (e + 1) * C)
             multiply(2, e, False, True)
             nc.scalar.copy(y[:, e * C : (e + 1) * C], acc[e][:])
 

@@ -19,8 +19,6 @@ P = 128
 PASSES = K // 512
 SLOTS = E * C
 
-W_PIECE = 128
-SCALAR_LOW = (0, 1)
 X_ORDER = ((1, 0), (1, 1), (0, 0), (1, 2), (1, 3), (3, 0), (3, 1), (3, 2), (3, 3), (2, 0), (2, 1), (2, 2), (2, 3), (0, 1), (0, 2), (0, 3))
 
 def tile_routed_moe_kernel(tc, xT, w, gate, offs, pos1, pos2, out):
@@ -37,10 +35,7 @@ def tile_routed_moe_kernel(tc, xT, w, gate, offs, pos1, pos2, out):
 
         x_view = xT.rearrange("(g p j) n -> g p j n", g=PASSES, p=P, j=4)
         w_view = w.rearrange("e (g p j) n -> g p e (j n)", g=PASSES, p=P, j=4)
-        raw = {}
-        for g in (0, 1, 3):
-            raw[g] = keep.tile([P, 4, T], F32, name="raw%d" % g)
-        raw[2] = keep.tile([P, 4, T], F32, name="raw2", tag="slot_a", align_bytes=64)
+        raw = [keep.tile([P, 4, T], F32, name="raw%d" % g) for g in range(PASSES)]
         wraw = [keep.tile([P, E, 4 * N], F32, name="wraw%d" % g) for g in range(PASSES)]
 
         def load_x(g, j):
@@ -68,18 +63,18 @@ def tile_routed_moe_kernel(tc, xT, w, gate, offs, pos1, pos2, out):
         for g in (1, 2, 3):
             xb[g] = keep.tile([P, 4, T], BF16, name="xb%d" % g)
         quad = {}
-        quad[0] = keep.tile([P, 4 * SLOTS], BF16, name="quad0", align_bytes=64)
-        quad[2] = keep.tile([P, 4 * SLOTS], BF16, name="quad2", align_bytes=64)
-        wquad = [keep.tile([P, 4 * E * N], BF16, name="wquad%d" % g, align_bytes=64) for g in range(PASSES)]
+        quad[0] = keep.tile([P, 4 * SLOTS], BF16, name="quad0", tag="slot_b", align_bytes=64)
+        wquad = {}
         x_codes = keep.tile([P, PASSES, SLOTS], U32, name="x_codes", align_bytes=64)
         x_scales = keep.tile([P, PASSES, SLOTS], U8, name="x_scales", align_bytes=64)
+        w_codes = keep.tile([P, PASSES, E * N], U32, name="w_codes", align_bytes=64)
         w_scales = keep.tile([P, PASSES, E * N], U8, name="w_scales", align_bytes=64)
         acc = [psum.tile([P, C], F32, name="acc%d" % e) for e in range(E)]
         y = keep.tile([P, SLOTS], F32, name="y")
         pairs = {}
-        for g in (0, 1):
+        for g in (1, 3):
             pairs[g] = keep.tile([P, 2, 2 * SLOTS], BF16, name="pairs%d" % g)
-        pairs[3] = keep.tile([P, 2, 2 * SLOTS], BF16, name="pairs3", tag="slot_b", align_bytes=64)
+        pairs[0] = keep.tile([P, 2, 2 * SLOTS], BF16, name="pairs0", tag="slot_a", align_bytes=64)
         units = [keep.tile([P, 2, 2 * C], BF16, name="unit%d" % e) for e in range(E)]
 
         def cast(g, j):
@@ -114,47 +109,16 @@ def tile_routed_moe_kernel(tc, xT, w, gate, offs, pos1, pos2, out):
             )
 
         def prep_w(g):
-            dst = wquad[g][:].rearrange("p (e n j) -> p e n j", e=E, j=4)
-            src = wraw[g][:].rearrange("p e (j n) -> p e n j", j=4)
-            for e in range(E):
-                for h in range(0, N, W_PIECE):
-                    nc.gpsimd.tensor_scalar(dst[:, e, h : h + W_PIECE], src[:, e, h : h + W_PIECE], 1.0, 0.0, MULT, ADD)
+            nc.vector.tensor_copy(
+                wquad[g // 2][:, g % 2, :].rearrange("p (e n j) -> p e n j", e=E, j=4),
+                wraw[g][:].rearrange("p e (j n) -> p e n j", j=4),
+            )
 
-        for g in range(PASSES):
-            prep_w(g)
-
-        for g, j in X_ORDER:
-            if g == 0:
-                plane("vector", 0, j)
-            elif g == 2:
-                if j > 1 or SCALAR_LOW:
-                    cast(2, j)
-            else:
-                cast(g, j)
-                plane("scalar", g, j)
-        for e in range(E):
-            for j in range(4):
-                if j > 1 or e in SCALAR_LOW:
-                    gather("scalar", 2, e, j)
-        for e in range(E):
-            for j in (0, 1):
-                if e not in SCALAR_LOW:
-                    gather("vector", 2, e, j)
-
-        merge(0, pairs[0], 0, SLOTS)
-        quad[1] = keep.tile([P, 4 * SLOTS], BF16, name="quad1", tag="slot_a", align_bytes=64)
-        merge(1, pairs[1], 0, SLOTS)
-        quant_x(0, 0, SLOTS)
-        quant_x(1, 0, SLOTS)
-        quad[3] = keep.tile([P, 4 * SLOTS], BF16, name="quad3", tag="slot_a", align_bytes=64)
-        merge(3, pairs[3], 0, SLOTS)
-        quant_x(3, 0, SLOTS)
-        w_codes = keep.tile([P, PASSES, E * N], U32, name="w_codes", tag="slot_b", align_bytes=64)
-        for g in range(PASSES):
+        def quant_w(h):
             nc.vector.quantize_mx(
-                out=w_codes[:, g, :].bitcast(FP8X4),
-                scales=w_scales[:, g, :],
-                in_=wquad[g][:],
+                out=w_codes[:, 2 * h : 2 * h + 2, :].rearrange("p a b -> p (a b)").bitcast(FP8X4),
+                scales=w_scales[:, 2 * h : 2 * h + 2, :].rearrange("p a b -> p (a b)"),
+                in_=wquad[h][:].rearrange("p a b -> p (a b)"),
             )
 
         def multiply(g, e, first, last):
@@ -168,9 +132,39 @@ def tile_routed_moe_kernel(tc, xT, w, gate, offs, pos1, pos2, out):
                 stop=last,
             )
 
+        for g, j in X_ORDER:
+            if g == 0:
+                plane("vector", 0, j)
+            elif g == 2:
+                cast(2, j)
+            else:
+                cast(g, j)
+                plane("scalar", g, j)
+        for e in range(E):
+            for j in range(4):
+                gather("scalar", 2, e, j)
+
+        merge(0, pairs[0], 0, SLOTS)
+        quad[1] = keep.tile([P, 4 * SLOTS], BF16, name="quad1", tag="slot_a", align_bytes=64)
+        merge(1, pairs[1], 0, SLOTS)
+        quant_x(0, 0, SLOTS)
+        quant_x(1, 0, SLOTS)
+        wquad[0] = keep.tile([P, 2, 4 * E * N], BF16, name="wquad01", tag="slot_b", align_bytes=64)
+        wquad[1] = keep.tile([P, 2, 4 * E * N], BF16, name="wquad23", tag="slot_a", align_bytes=64)
+        prep_w(0)
+        prep_w(1)
+        prep_w(2)
+        quant_w(0)
+        prep_w(3)
+        quant_w(1)
+        quad[3] = keep.tile([P, 4 * SLOTS], BF16, name="quad3", tag="slot_a", align_bytes=64)
+        merge(3, pairs[3], 0, SLOTS)
+        quant_x(3, 0, SLOTS)
+
         for g in (0, 1, 3):
             for e in range(E):
                 multiply(g, e, g == 0, False)
+        quad[2] = keep.tile([P, 4 * SLOTS], BF16, name="quad2", tag="slot_a", align_bytes=64)
         for e in range(E):
             merge(2, units[e], e * C, (e + 1) * C)
             quant_x(2, e * C, (e + 1) * C)

@@ -19,7 +19,14 @@ P = 128
 PASSES = K // 512
 SLOTS = E * C
 
-X_ORDER = ((1, 0), (1, 1), (0, 0), (1, 2), (1, 3), (3, 0), (3, 1), (3, 2), (3, 3), (2, 0), (2, 1), (2, 2), (2, 3), (0, 1), (0, 2), (0, 3))
+VECTOR_OF_PASS_2 = ()
+X_ORDER = ((1, 0), (1, 1), (0, 0), (1, 2), (1, 3), (0, 1), (3, 0), (3, 1), (0, 2), (3, 2), (3, 3), (0, 3), (2, 0), (2, 1), (2, 2), (2, 3))
+W_ORDER = tuple((g, e) for g in range(PASSES) for e in range(E))
+LOAD_ORDER = tuple(
+    item
+    for i in range(len(X_ORDER))
+    for item in ([("x",) + X_ORDER[i]] + ([("w",) + W_ORDER[(i - 2) // 2]] if i >= 2 and i % 2 == 0 else []))
+) + tuple(("w",) + W_ORDER[i] for i in range(7, len(W_ORDER)))
 
 def tile_routed_moe_kernel(tc, xT, w, gate, offs, pos1, pos2, out):
     nc = tc.nc
@@ -38,17 +45,11 @@ def tile_routed_moe_kernel(tc, xT, w, gate, offs, pos1, pos2, out):
         raw = [keep.tile([P, 4, T], F32, name="raw%d" % g) for g in range(PASSES)]
         wraw = [keep.tile([P, E, 4 * N], F32, name="wraw%d" % g) for g in range(PASSES)]
 
-        def load_x(g, j):
-            nc.sync.dma_start(raw[g][:, j, :], x_view[g, :, j, :])
-
-        def load_w(g):
-            for e in range(E):
-                nc.sync.dma_start(wraw[g][:, e, :], w_view[g, :, e, :])
-
-        for g, j in X_ORDER:
-            load_x(g, j)
-        for g in range(PASSES):
-            load_w(g)
+        for kind, g, k in LOAD_ORDER:
+            if kind == "x":
+                nc.sync.dma_start(raw[g][:, k, :], x_view[g, :, k, :])
+            else:
+                nc.sync.dma_start(wraw[g][:, k, :], w_view[g, :, k, :])
         gate_t = keep.tile([P, 2, T], F32, name="gate_t")
         nc.sync.dma_start(gate_t[:], gate.rearrange("r n t -> n r t"))
         nc.sync.dma_start(pos1_t[:], pos1)
@@ -63,18 +64,17 @@ def tile_routed_moe_kernel(tc, xT, w, gate, offs, pos1, pos2, out):
         for g in (1, 2, 3):
             xb[g] = keep.tile([P, 4, T], BF16, name="xb%d" % g)
         quad = {}
-        quad[0] = keep.tile([P, 4 * SLOTS], BF16, name="quad0", tag="slot_b", align_bytes=64)
-        wquad = {}
+        quad[0] = keep.tile([P, 4 * SLOTS], BF16, name="quad0", align_bytes=64)
+        wquad = [keep.tile([P, 4 * E * N], BF16, name="wquad%d" % g, align_bytes=64) for g in range(PASSES)]
         x_codes = keep.tile([P, PASSES, SLOTS], U32, name="x_codes", align_bytes=64)
         x_scales = keep.tile([P, PASSES, SLOTS], U8, name="x_scales", align_bytes=64)
-        w_codes = keep.tile([P, PASSES, E * N], U32, name="w_codes", align_bytes=64)
         w_scales = keep.tile([P, PASSES, E * N], U8, name="w_scales", align_bytes=64)
         acc = [psum.tile([P, C], F32, name="acc%d" % e) for e in range(E)]
         y = keep.tile([P, SLOTS], F32, name="y")
         pairs = {}
-        for g in (1, 3):
-            pairs[g] = keep.tile([P, 2, 2 * SLOTS], BF16, name="pairs%d" % g)
+        pairs[1] = keep.tile([P, 2, 2 * SLOTS], BF16, name="pairs1")
         pairs[0] = keep.tile([P, 2, 2 * SLOTS], BF16, name="pairs0", tag="slot_a", align_bytes=64)
+        pairs[3] = keep.tile([P, 2, 2 * SLOTS], BF16, name="pairs3", tag="slot_b", align_bytes=64)
         units = [keep.tile([P, 2, 2 * C], BF16, name="unit%d" % e) for e in range(E)]
 
         def cast(g, j):
@@ -108,28 +108,11 @@ def tile_routed_moe_kernel(tc, xT, w, gate, offs, pos1, pos2, out):
                 in_=quad[g][:, 4 * a : 4 * b],
             )
 
-        def prep_w(g):
-            nc.vector.tensor_copy(
-                wquad[g // 2][:, g % 2, :].rearrange("p (e n j) -> p e n j", e=E, j=4),
-                wraw[g][:].rearrange("p e (j n) -> p e n j", j=4),
-            )
-
-        def quant_w(h):
-            nc.vector.quantize_mx(
-                out=w_codes[:, 2 * h : 2 * h + 2, :].rearrange("p a b -> p (a b)").bitcast(FP8X4),
-                scales=w_scales[:, 2 * h : 2 * h + 2, :].rearrange("p a b -> p (a b)"),
-                in_=wquad[h][:].rearrange("p a b -> p (a b)"),
-            )
-
-        def multiply(g, e, first, last):
-            nc.tensor.matmul_mx(
-                out=acc[e][:],
-                lhsT=w_codes[:, g, e * N : (e + 1) * N].bitcast(FP8X4),
-                lhsT_scale=w_scales[:, g, e * N : (e + 1) * N],
-                rhs=x_codes[:, g, e * C : (e + 1) * C].bitcast(FP8X4),
-                rhs_scale=x_scales[:, g, e * C : (e + 1) * C],
-                start=first,
-                stop=last,
+        for g, e in W_ORDER:
+            nc.gpsimd.tensor_scalar(
+                wquad[g][:].rearrange("p (e n j) -> p e n j", e=E, j=4)[:, e],
+                wraw[g][:].rearrange("p e (j n) -> p e n j", j=4)[:, e],
+                1.0, 0.0, MULT, ADD,
             )
 
         for g, j in X_ORDER:
@@ -142,24 +125,37 @@ def tile_routed_moe_kernel(tc, xT, w, gate, offs, pos1, pos2, out):
                 plane("scalar", g, j)
         for e in range(E):
             for j in range(4):
-                gather("scalar", 2, e, j)
+                if (e, j) not in VECTOR_OF_PASS_2:
+                    gather("scalar", 2, e, j)
+        for e, j in VECTOR_OF_PASS_2:
+            gather("vector", 2, e, j)
 
         merge(0, pairs[0], 0, SLOTS)
         quad[1] = keep.tile([P, 4 * SLOTS], BF16, name="quad1", tag="slot_a", align_bytes=64)
         merge(1, pairs[1], 0, SLOTS)
         quant_x(0, 0, SLOTS)
         quant_x(1, 0, SLOTS)
-        wquad[0] = keep.tile([P, 2, 4 * E * N], BF16, name="wquad01", tag="slot_b", align_bytes=64)
-        wquad[1] = keep.tile([P, 2, 4 * E * N], BF16, name="wquad23", tag="slot_a", align_bytes=64)
-        prep_w(0)
-        prep_w(1)
-        prep_w(2)
-        quant_w(0)
-        prep_w(3)
-        quant_w(1)
         quad[3] = keep.tile([P, 4 * SLOTS], BF16, name="quad3", tag="slot_a", align_bytes=64)
         merge(3, pairs[3], 0, SLOTS)
         quant_x(3, 0, SLOTS)
+        w_codes = keep.tile([P, PASSES, E * N], U32, name="w_codes", tag="slot_b", align_bytes=64)
+        for g in range(PASSES):
+            nc.vector.quantize_mx(
+                out=w_codes[:, g, :].bitcast(FP8X4),
+                scales=w_scales[:, g, :],
+                in_=wquad[g][:],
+            )
+
+        def multiply(g, e, first, last):
+            nc.tensor.matmul_mx(
+                out=acc[e][:],
+                lhsT=w_codes[:, g, e * N : (e + 1) * N].bitcast(FP8X4),
+                lhsT_scale=w_scales[:, g, e * N : (e + 1) * N],
+                rhs=x_codes[:, g, e * C : (e + 1) * C].bitcast(FP8X4),
+                rhs_scale=x_scales[:, g, e * C : (e + 1) * C],
+                start=first,
+                stop=last,
+            )
 
         for g in (0, 1, 3):
             for e in range(E):

@@ -19,7 +19,7 @@ P = 128
 PASSES = K // 512
 SLOTS = E * C
 
-VECTOR_OF_PASS_2 = ()
+VECTOR_OF_PASS_2 = ((3, 0), (3, 1))
 X_ORDER = ((1, 0), (1, 1), (0, 0), (1, 2), (1, 3), (0, 1), (3, 0), (3, 1), (0, 2), (3, 2), (3, 3), (0, 3), (2, 0), (2, 1), (2, 2), (2, 3))
 W_ORDER = tuple((g, e) for g in range(PASSES) for e in range(E))
 LOAD_ORDER = tuple(
@@ -64,8 +64,10 @@ def tile_routed_moe_kernel(tc, xT, w, gate, offs, pos1, pos2, out):
         for g in (1, 2, 3):
             xb[g] = keep.tile([P, 4, T], BF16, name="xb%d" % g)
         quad = {}
-        quad[0] = keep.tile([P, 4 * SLOTS], BF16, name="quad0", align_bytes=64)
-        wquad = [keep.tile([P, 4 * E * N], BF16, name="wquad%d" % g, align_bytes=64) for g in range(PASSES)]
+        quad[0] = keep.tile([P, 4 * SLOTS], BF16, name="quad0", tag="slot_c", align_bytes=64)
+        wquad = {}
+        for g in range(PASSES - 1):
+            wquad[g] = keep.tile([P, 4 * E * N], BF16, name="wquad%d" % g, align_bytes=64)
         x_codes = keep.tile([P, PASSES, SLOTS], U32, name="x_codes", align_bytes=64)
         x_scales = keep.tile([P, PASSES, SLOTS], U8, name="x_scales", align_bytes=64)
         w_scales = keep.tile([P, PASSES, E * N], U8, name="w_scales", align_bytes=64)
@@ -108,7 +110,7 @@ def tile_routed_moe_kernel(tc, xT, w, gate, offs, pos1, pos2, out):
                 in_=quad[g][:, 4 * a : 4 * b],
             )
 
-        for g, e in W_ORDER:
+        for g, e in W_ORDER[: (PASSES - 1) * E]:
             nc.gpsimd.tensor_scalar(
                 wquad[g][:].rearrange("p (e n j) -> p e n j", e=E, j=4)[:, e],
                 wraw[g][:].rearrange("p e (j n) -> p e n j", j=4)[:, e],
@@ -135,6 +137,11 @@ def tile_routed_moe_kernel(tc, xT, w, gate, offs, pos1, pos2, out):
         merge(1, pairs[1], 0, SLOTS)
         quant_x(0, 0, SLOTS)
         quant_x(1, 0, SLOTS)
+        wquad[3] = keep.tile([P, 4 * E * N], BF16, name="wquad3", tag="slot_c", align_bytes=64)
+        nc.vector.tensor_copy(
+            wquad[3][:].rearrange("p (e n j) -> p e n j", e=E, j=4),
+            wraw[3][:].rearrange("p e (j n) -> p e n j", j=4),
+        )
         quad[3] = keep.tile([P, 4 * SLOTS], BF16, name="quad3", tag="slot_a", align_bytes=64)
         merge(3, pairs[3], 0, SLOTS)
         quant_x(3, 0, SLOTS)

@@ -20,7 +20,7 @@ PASSES = K // 512
 SLOTS = E * C
 
 VECTOR_OF_PASS_2 = ((3, 0), (3, 1))
-X_ORDER = ((1, 0), (1, 1), (0, 0), (1, 2), (1, 3), (0, 1), (3, 0), (3, 1), (0, 2), (3, 2), (3, 3), (0, 3), (2, 0), (2, 1), (2, 2), (2, 3))
+X_ORDER = ((1, 0), (1, 1), (0, 0), (1, 2), (1, 3), (0, 1), (3, 0), (3, 1), (3, 2), (3, 3), (0, 2), (0, 3), (2, 0), (2, 1), (2, 2), (2, 3))
 W_ORDER = tuple((g, e) for g in range(PASSES) for e in range(E))
 LOAD_ORDER = tuple(
     item
@@ -79,8 +79,8 @@ def tile_routed_moe_kernel(tc, xT, w, gate, offs, pos1, pos2, out):
         pairs[3] = keep.tile([P, 2, 2 * SLOTS], BF16, name="pairs3", tag="slot_b", align_bytes=64)
         units = [keep.tile([P, 2, 2 * C], BF16, name="unit%d" % e) for e in range(E)]
 
-        def cast(g, j):
-            nc.vector.tensor_copy(xb[g][:, j, :], raw[g][:, j, :])
+        def cast(g, a, b):
+            nc.vector.tensor_copy(xb[g][:, a:b, :], raw[g][:, a:b, :])
 
         def gather(engine, g, e, j):
             if g == 2:
@@ -117,14 +117,21 @@ def tile_routed_moe_kernel(tc, xT, w, gate, offs, pos1, pos2, out):
                 1.0, 0.0, MULT, ADD,
             )
 
-        for g, j in X_ORDER:
-            if g == 0:
-                plane("vector", 0, j)
-            elif g == 2:
-                cast(2, j)
-            else:
-                cast(g, j)
-                plane("scalar", g, j)
+        cast(1, 0, 1)
+        plane("scalar", 1, 0)
+        cast(1, 1, 2)
+        plane("scalar", 1, 1)
+        plane("vector", 0, 0)
+        cast(1, 2, 4)
+        plane("scalar", 1, 2)
+        plane("scalar", 1, 3)
+        plane("vector", 0, 1)
+        cast(3, 0, 4)
+        for j in range(4):
+            plane("scalar", 3, j)
+        plane("vector", 0, 2)
+        plane("vector", 0, 3)
+        cast(2, 0, 4)
         for e in range(E):
             for j in range(4):
                 if (e, j) not in VECTOR_OF_PASS_2:

@@ -20,6 +20,7 @@ PASSES = K // 512
 SLOTS = E * C
 
 VECTOR_OF_PASS_2 = ((3, 0), (3, 1))
+W_ON_GPSIMD = 10
 X_ORDER = ((1, 0), (1, 1), (0, 0), (1, 2), (1, 3), (0, 1), (3, 0), (3, 1), (3, 2), (3, 3), (0, 2), (0, 3), (2, 0), (2, 1), (2, 2), (2, 3))
 W_ORDER = tuple((g, e) for g in range(PASSES) for e in range(E))
 LOAD_ORDER = tuple(
@@ -110,7 +111,7 @@ def tile_routed_moe_kernel(tc, xT, w, gate, offs, pos1, pos2, out):
                 in_=quad[g][:, 4 * a : 4 * b],
             )
 
-        for g, e in W_ORDER[: (PASSES - 1) * E]:
+        for g, e in W_ORDER[:W_ON_GPSIMD]:
             nc.gpsimd.tensor_scalar(
                 wquad[g][:].rearrange("p (e n j) -> p e n j", e=E, j=4)[:, e],
                 wraw[g][:].rearrange("p e (j n) -> p e n j", j=4)[:, e],
@@ -144,6 +145,10 @@ def tile_routed_moe_kernel(tc, xT, w, gate, offs, pos1, pos2, out):
         merge(1, pairs[1], 0, SLOTS)
         quant_x(0, 0, SLOTS)
         quant_x(1, 0, SLOTS)
+        nc.vector.tensor_copy(
+            wquad[2][:].rearrange("p (e n j) -> p e n j", e=E, j=4)[:, W_ON_GPSIMD - 2 * E :],
+            wraw[2][:].rearrange("p e (j n) -> p e n j", j=4)[:, W_ON_GPSIMD - 2 * E :],
+        )
         wquad[3] = keep.tile([P, 4 * E * N], BF16, name="wquad3", tag="slot_c", align_bytes=64)
         nc.vector.tensor_copy(
             wquad[3][:].rearrange("p (e n j) -> p e n j", e=E, j=4),

from contextlib import ExitStack

import concourse.mybir as mybir

K, T, E, C, N = 2048, 512, 4, 256, 128
FLOPS = 2 * K * N * E * C

F32 = mybir.dt.float32
BF16 = mybir.dt.bfloat16
U32 = mybir.dt.uint32
U16 = mybir.dt.uint16
U8 = mybir.dt.uint8
FP8X4 = mybir.dt.float8_e4m3fn_x4
MULT = mybir.AluOpType.mult
ADD = mybir.AluOpType.add
COPY = mybir.ActivationFunctionType.Copy

P = 128
PASSES = K // 512
SLOTS = E * C

VECTOR_OF_PASS_2 = ((3, 0), (3, 1))
W_ON_GPSIMD = 10
X_ORDER = ((1, 0), (1, 1), (0, 0), (1, 2), (1, 3), (0, 1), (3, 0), (3, 1), (3, 2), (3, 3), (0, 2), (0, 3), (2, 0), (2, 1), (2, 2), (2, 3))
W_ORDER = tuple((g, e) for g in range(PASSES) for e in range(E))
LOAD_ORDER = tuple(
    item
    for i in range(len(X_ORDER))
    for item in ([("x",) + X_ORDER[i]] + ([("w",) + W_ORDER[(i - 2) // 2]] if i >= 2 and i % 2 == 0 else []))
) + tuple(("w",) + W_ORDER[i] for i in range(7, len(W_ORDER)))

def tile_routed_moe_kernel(tc, xT, w, gate, offs, pos1, pos2, out):
    nc = tc.nc
    with ExitStack() as ctx:
        lists = ctx.enter_context(tc.tile_pool(name="lists", bufs=1))
        keep = ctx.enter_context(tc.tile_pool(name="keep", bufs=1))
        psum = ctx.enter_context(tc.psum_pool(name="psum", bufs=1))

        offs_t = lists.tile([P, SLOTS // 16], U16, name="offs_t")
        pos1_t = lists.tile([P, T // 16], U16, name="pos1_t")
        pos2_t = lists.tile([P, T // 16], U16, name="pos2_t")
        nc.sync.dma_start(offs_t[:], offs)

        x_view = xT.rearrange("(g p j) n -> g p j n", g=PASSES, p=P, j=4)
        w_view = w.rearrange("e (g p j) n -> g p e (j n)", g=PASSES, p=P, j=4)
        raw = [keep.tile([P, 4, T], F32, name="raw%d" % g) for g in range(PASSES)]
        wraw = [keep.tile([P, E, 4 * N], F32, name="wraw%d" % g) for g in range(PASSES)]

        for kind, g, k in LOAD_ORDER:
            if kind == "x":
                nc.sync.dma_start(raw[g][:, k, :], x_view[g, :, k, :])
            else:
                nc.sync.dma_start(wraw[g][:, k, :], w_view[g, :, k, :])
        gate_t = keep.tile([P, 2, T], F32, name="gate_t")
        nc.sync.dma_start(gate_t[:], gate.rearrange("r n t -> n r t"))
        nc.sync.dma_start(pos1_t[:], pos1)
        nc.sync.dma_start(pos2_t[:], pos2)

        zero = keep.tile([P, 1], F32, name="zero")
        warm = keep.tile([P, 1], F32, name="warm")
        nc.vector.memset(zero[:], 0.0)
        nc.scalar.copy(warm[:], zero[:])

        xb = {}
        for g in (1, 2, 3):
            xb[g] = keep.tile([P, 4, T], BF16, name="xb%d" % g)
        quad = {}
        quad[0] = keep.tile([P, 4 * SLOTS], BF16, name="quad0", tag="slot_c", align_bytes=64)
        wquad = {}
        for g in range(PASSES - 1):
            wquad[g] = keep.tile([P, 4 * E * N], BF16, name="wquad%d" % g, align_bytes=64)
        x_codes = keep.tile([P, PASSES, SLOTS], U32, name="x_codes", align_bytes=64)
        x_scales = keep.tile([P, PASSES, SLOTS], U8, name="x_scales", align_bytes=64)
        w_scales = keep.tile([P, PASSES, E * N], U8, name="w_scales", align_bytes=64)
        acc = [psum.tile([P, C], F32, name="acc%d" % e) for e in range(E)]
        y = keep.tile([P, SLOTS], F32, name="y")
        pairs = {}
        pairs[1] = keep.tile([P, 2, 2 * SLOTS], BF16, name="pairs1")
        pairs[0] = keep.tile([P, 2, 2 * SLOTS], BF16, name="pairs0", tag="slot_a", align_bytes=64)
        pairs[3] = keep.tile([P, 2, 2 * SLOTS], BF16, name="pairs3", tag="slot_b", align_bytes=64)
        units = [keep.tile([P, 2, 2 * C], BF16, name="unit%d" % e) for e in range(E)]

        def cast(g, a, b):
            nc.vector.tensor_copy(xb[g][:, a:b, :], raw[g][:, a:b, :])

        def gather(engine, g, e, j):
            if g == 2:
                dst = units[e][:, j // 2, :].rearrange("p (n i) -> p n i", i=2)[:, :, j % 2]
            else:
                dst = pairs[g][:, j // 2, :].rearrange("p (n i) -> p n i", i=2)[:, e * C : (e + 1) * C, j % 2]
            cols = offs_t[:, e * C // 16 : (e + 1) * C // 16]
            if engine == "vector":
                nc.vector.tensor_copy(dst, raw[g][:, j, :].indirect(cols))
            else:
                nc.scalar.activation(dst, xb[g][:, j, :].indirect(cols), COPY)

        def plane(engine, g, j):
            for e in range(E):
                gather(engine, g, e, j)

        def merge(g, src, a, b):
            nc.vector.tensor_copy(
                quad[g][:].bitcast(F32)[:, 2 * a : 2 * b].rearrange("p (n u) -> p n u", u=2),
                src[:].bitcast(F32).rearrange("p u n -> p n u"),
            )

        def quant_x(g, a, b):
            nc.vector.quantize_mx(
                out=x_codes[:, g, a:b].bitcast(FP8X4),
                scales=x_scales[:, g, a:b],
                in_=quad[g][:, 4 * a : 4 * b],
            )

        for g, e in W_ORDER[:W_ON_GPSIMD]:
            nc.gpsimd.tensor_scalar(
                wquad[g][:].rearrange("p (e n j) -> p e n j", e=E, j=4)[:, e],
                wraw[g][:].rearrange("p e (j n) -> p e n j", j=4)[:, e],
                1.0, 0.0, MULT, ADD,
            )

        cast(1, 0, 1)
        plane("scalar", 1, 0)
        cast(1, 1, 2)
        plane("scalar", 1, 1)
        plane("vector", 0, 0)
        cast(1, 2, 4)
        plane("scalar", 1, 2)
        plane("scalar", 1, 3)
        plane("vector", 0, 1)
        cast(3, 0, 4)
        for j in range(4):
            plane("scalar", 3, j)
        plane("vector", 0, 2)
        plane("vector", 0, 3)
        cast(2, 0, 4)
        for e in range(E):
            for j in range(4):
                if (e, j) not in VECTOR_OF_PASS_2:
                    gather("scalar", 2, e, j)
        for e, j in VECTOR_OF_PASS_2:
            gather("vector", 2, e, j)

        merge(0, pairs[0], 0, SLOTS)
        quad[1] = keep.tile([P, 4 * SLOTS], BF16, name="quad1", tag="slot_a", align_bytes=64)
        merge(1, pairs[1], 0, SLOTS)
        quant_x(0, 0, SLOTS)
        quant_x(1, 0, SLOTS)
        nc.vector.tensor_copy(
            wquad[2][:].rearrange("p (e n j) -> p e n j", e=E, j=4)[:, W_ON_GPSIMD - 2 * E :],
            wraw[2][:].rearrange("p e (j n) -> p e n j", j=4)[:, W_ON_GPSIMD - 2 * E :],
        )
        wquad[3] = keep.tile([P, 4 * E * N], BF16, name="wquad3", tag="slot_c", align_bytes=64)
        nc.vector.tensor_copy(
            wquad[3][:].rearrange("p (e n j) -> p e n j", e=E, j=4),
            wraw[3][:].rearrange("p e (j n) -> p e n j", j=4),
        )
        quad[3] = keep.tile([P, 4 * SLOTS], BF16, name="quad3", tag="slot_a", align_bytes=64)
        merge(3, pairs[3], 0, SLOTS)
        quant_x(3, 0, SLOTS)
        w_codes = keep.tile([P, PASSES, E * N], U32, name="w_codes", tag="slot_b", align_bytes=64)
        for g in range(PASSES):
            nc.vector.quantize_mx(
                out=w_codes[:, g, :].bitcast(FP8X4),
                scales=w_scales[:, g, :],
                in_=wquad[g][:],
            )

        def multiply(g, e, first, last):
            nc.tensor.matmul_mx(
                out=acc[e][:],
                lhsT=w_codes[:, g, e * N : (e + 1) * N].bitcast(FP8X4),
                lhsT_scale=w_scales[:, g, e * N : (e + 1) * N],
                rhs=x_codes[:, g, e * C : (e + 1) * C].bitcast(FP8X4),
                rhs_scale=x_scales[:, g, e * C : (e + 1) * C],
                start=first,
                stop=last,
            )

        for g in (0, 1, 3):
            for e in range(E):
                multiply(g, e, g == 0, False)
        quad[2] = keep.tile([P, 4 * SLOTS], BF16, name="quad2", tag="slot_a", align_bytes=64)
        for e in range(E):
            merge(2, units[e], e * C, (e + 1) * C)
            quant_x(2, e * C, (e + 1) * C)
            multiply(2, e, False, True)
            nc.scalar.copy(y[:, e * C : (e + 1) * C], acc[e][:])

        part1 = keep.tile([P, T], F32, name="part1")
        part2 = keep.tile([P, T], F32, name="part2")
        total = keep.tile([P, T], F32, name="total")
        nc.vector.tensor_tensor(part1[:], y[:].indirect(pos1_t[:]), gate_t[:, 0, :], MULT)
        nc.vector.tensor_tensor(part2[:], y[:].indirect(pos2_t[:]), gate_t[:, 1, :], MULT)
        nc.vector.tensor_tensor(total[:], part1[:], part2[:], ADD)
        nc.sync.dma_start(out, total[:])
